import numpy as np
CORES = [144,200,272,328,400,456]
N = 6
F = 64
def setup_inputs(rng):
    return {"gr": rng.standard_normal((N, 128, F), dtype=np.float32) * (0.5 + np.abs(rng.standard_normal((1, 128, 1), dtype=np.float32))) * (0.5 + np.abs(rng.standard_normal((N, 1, F), dtype=np.float32)))}
def setup_inputs_big(rng):
    d = setup_inputs(rng)
    for k in ("gr",): d[k] = (d[k].astype(np.float32) * 1024.0).astype(d[k].dtype)
    return d
def setup_inputs_small(rng):
    d = setup_inputs(rng)
    for k in ("gr",): d[k] = (d[k].astype(np.float32) * (1 / 1024.0)).astype(d[k].dtype)
    return d
def setup_inputs_apart(rng):
    d = setup_inputs(rng)
    f = (10.0 ** rng.permutation(np.linspace(-1.5, 1.5, N))).astype(np.float32).reshape(N, 1, 1)
    for k in ("gr",): d[k] = (d[k].astype(np.float32) * f).astype(d[k].dtype)
    return d
def setup_inputs_mixed(rng):
    d = setup_inputs(rng)
    f = (10.0 ** rng.uniform(-3, 3, (1, 128, 1)) * 10.0 ** rng.uniform(-3, 3, (N, 1, F))).astype(np.float32)
    for k in ("gr",): d[k] = (d[k].astype(np.float32) * f).astype(d[k].dtype)
    return d
def reference(gr):
    G = gr.astype(np.float64); G2 = G ** 2
    R = G2.sum(axis=(0, 2)).reshape(1, 128, 1) / (N * F)
    Cm = G2.sum(axis=1, keepdims=True) / 128
    M = R.sum() / 128
    return {"y": (G / np.sqrt(R * Cm / M)).astype(np.float32)}

from concourse.bass import DstId, RemoteDMATransfer
from concourse.mybir import AluOpType, AxisListType, ActivationFunctionType
import comms_topo

CORES = [144, 200, 272, 328, 400, 456]
P, F = 128, 64
WORLD = 4 * comms_topo.CORES_PER_HOST
SEND_ENGINES = 4
HUB_ENGINES = 2


def _same_chip(a, b):
    return comms_topo.host(a) == comms_topo.host(b) and comms_topo.chip(a) == comms_topo.chip(b)


def _plan():
    free = [c for c in range(WORLD) if c not in CORES and all(comms_topo.may_write(c, r) for r in CORES)]
    left, hubs = list(CORES), []
    while left:
        def score(c):
            mine = [r for r in left if comms_topo.may_write(r, c)]
            return (len(mine), sum(_same_chip(r, c) for r in mine),
                    sum(comms_topo.die(r) == comms_topo.die(c) for r in mine))
        hub = max(free, key=score)
        mine = [r for r in left if comms_topo.may_write(r, hub)]
        hubs.append((hub, mine))
        left = [r for r in left if r not in mine]
        free.remove(hub)
    return hubs


HUBS = _plan()
H = len(HUBS)
SLOTS = max(len(mine) for _, mine in HUBS)

SCRATCH = {
    "gin": ("sbuf", [P, F], "float32"),
    "g2": ("sbuf", [P, F], "float32"),
    "rs": ("sbuf", [P, 1], "float32"),
    "ones": ("sbuf", [P, P], "float32"),
    "hub_in": ("dram", [SLOTS, P, 1], "float32"),
    "land": ("dram", [H, P, 1], "float32"),
    "landT": ("sbuf", [H, P], "float32"),
    "tot": ("sbuf", [H, 1], "float32"),
    "cr": ("sbuf", [P, F], "float32"),
    "ct": ("sbuf", [P, F], "float32"),
    "gsc": ("sbuf", [P, F], "float32"),
    "rinv": ("sbuf", [P, 1], "float32"),
    "rw": ("sbuf", [P, 1], "float32"),
    "yo": ("sbuf", [P, F], "float32"),
    "cs_ps": ("psum", [P, 512], "float32"),
    "r_ps": ("psum", [P, 512], "float32"),
    "m_ps": ("psum", [P, 512], "float32"),
}
SEMAPHORES = ["ld", "one", "sq", "sent", "harr", "arr", "cs", "c1", "v", "lt", "rp", "ts", "mp", "ri", "rw", "yy", "st"]


def _engines(mask, n):
    return [1 << b for b in range(16) if (mask >> b) & 1][:n]


def _hub_program(g, core, T, topo, h, mine):
    s = T.sem
    g.wait_ge(s.harr, SEND_ENGINES * len(mine))
    allowed = ~0
    for r in T.cores:
        allowed &= topo.mask(core, r)
    engines = _engines(allowed, HUB_ENGINES)
    dests = sorted(T.cores, key=lambda r: _same_chip(r, core))
    srcs = [T.hub_in[k] for k in range(len(mine))]
    transfers = []
    for e, m in enumerate(engines):
        part = dests[e::len(engines)]
        ids = [topo.addr(r, core) for r in part]
        transfers.append(RemoteDMATransfer(dst_ids=[DstId(rid=rid, pnc=pid) for rid, pid in ids], dma_engine_mask=m,
                                           remote_sem=s.arr, srcs=srcs, dsts=[T.land[h] for _ in part], alu_op=1))
    g.remote_dma_fused(transfers, local_sem=s.sent)
    g.wait_ge(s.sent, len(engines))


def rank_program(g, core, T, topo):
    for h, (hub, mine) in enumerate(HUBS):
        if core == hub:
            _hub_program(g, core, T, topo, h, mine)
    if T.rank_of(core) is None:
        return
    s = T.sem
    Act, Op = ActivationFunctionType, AluOpType
    hub, mine = [(hub, mine) for hub, mine in HUBS if core in mine][0]

    g.vector.memset(T.ones[:, :], 1.0).then_inc(s.one, 1)
    g.sync.dma_start(T.gin[:, :], T.gr[:, :]).then_inc(s.ld, 16)
    g.scalar.wait_ge(s.ld, 16)
    g.scalar.activation(T.g2[:, :], T.gin[:, :], Act.Square, accum_out=T.rs[:, 0:1]).then_inc(s.sq, 1)
    g.wait_ge(s.sq, 1)
    rid, pid = topo.addr(hub, core)
    send_mask = sum(_engines(topo.mask(core, hub), SEND_ENGINES))
    g.remote_dma(out_ap=T.hub_in[mine.index(core)], in_ap=T.rs[:, 0:1], remote_sem=s.harr, local_sem=s.sent,
                 pid=pid, routing_id=rid, dma_engine_mask=send_mask)

    g.tensor.wait_ge(s.one, 1)
    g.tensor.wait_ge(s.sq, 1)
    g.tensor.matmul(T.cs_ps[:, 0:F], T.ones[:, :], T.g2[:, :], True, True).then_inc(s.cs, 1)
    g.scalar.wait_ge(s.cs, 1)
    g.scalar.activation(T.cr[:, :], T.cs_ps[:, 0:F], Act.Sqrt).then_inc(s.c1, 1)
    g.vector.wait_ge(s.c1, 1)
    g.vector.reciprocal(T.cr[:, :], T.cr[:, :]).then_inc(s.v, 1)
    g.vector.wait_ge(s.v, 1)
    g.vector.tensor_tensor(T.ct[:, :], T.cr[:, :], T.cs_ps[:, 0:F], Op.mult).then_inc(s.v, 1)
    g.vector.wait_ge(s.v, 2)
    g.vector.tensor_tensor(T.ct[:, :], T.ct[:, :], T.cr[:, :], Op.mult).then_inc(s.v, 1)
    g.vector.wait_ge(s.v, 3)
    g.vector.tensor_scalar(T.ct[:, :], T.ct[:, :], -0.5, 1.5, Op.mult, Op.add).then_inc(s.v, 1)
    g.vector.wait_ge(s.v, 4)
    g.vector.tensor_tensor(T.ct[:, :], T.ct[:, :], T.cr[:, :], Op.mult).then_inc(s.v, 1)
    g.vector.wait_ge(s.v, 5)
    g.vector.tensor_tensor(T.gsc[:, :], T.gin[:, :], T.ct[:, :], Op.mult).then_inc(s.v, 1)

    g.sync.wait_ge(s.arr, H)
    g.sync.dma_start(T.landT[:, :], T.land[:, :, 0]).then_inc(s.lt, 16)
    g.tensor.wait_ge(s.lt, 16)
    g.tensor.matmul(T.r_ps[:, 0:1], T.landT[:, :], T.ones[0:H, 0:1], True, True).then_inc(s.rp, 1)
    g.vector.wait_ge(s.lt, 16)
    g.vector.tensor_reduce(T.tot[:, 0:1], T.landT[:, :], AxisListType.X, Op.add).then_inc(s.ts, 1)
    g.tensor.wait_ge(s.ts, 1)
    g.tensor.matmul(T.m_ps[:, 0:1], T.ones[0:H, :], T.tot[:, 0:1], True, True).then_inc(s.mp, 1)
    g.vector.wait_ge(s.rp, 1)
    g.vector.reciprocal(T.rinv[:, 0:1], T.r_ps[:, 0:1]).then_inc(s.ri, 1)

    g.scalar.wait_ge(s.mp, 1)
    g.scalar.wait_ge(s.ri, 1)
    g.scalar.activation(T.rw[:, 0:1], T.m_ps[:, 0:1], Act.Sqrt, scale=T.rinv[:, 0:1]).then_inc(s.rw, 1)
    g.scalar.wait_ge(s.rw, 1)
    g.scalar.wait_ge(s.v, 6)
    g.scalar.activation(T.yo[:, :], T.gsc[:, :], Act.Copy, scale=T.rw[:, 0:1]).then_inc(s.yy, 1)
    g.scalar.wait_ge(s.yy, 1)
    g.scalar.dma_start(T.y[:, :], T.yo[:, :]).then_inc(s.st, 16)
    g.scalar.wait_ge(s.st, 16)
    g.wait_ge(s.sent, SEND_ENGINES)
